import numpy as np
import ml_dtypes


def mxq(x, axis, fmt="e4m3"):
    dtype, down = {"e4m3": (ml_dtypes.float8_e4m3fn, 7), "e5m2": (ml_dtypes.float8_e5m2, 14)}[fmt]
    v = np.moveaxis(np.asarray(x, np.float32).astype(ml_dtypes.bfloat16).astype(np.float64), axis, -1)
    blocks = v.reshape(v.shape[:-1] + (-1, 32))
    amax = np.abs(blocks).max(-1, keepdims=True)
    byte = np.maximum(np.where(amax > 0, np.frexp(amax)[1] - 1 + 127, 0) - down, 1)
    scale = np.exp2(byte - 127.0)
    codes = (blocks / scale).astype(np.float32).astype(dtype).astype(np.float64)
    return np.moveaxis((codes * scale).reshape(v.shape), -1, axis)


WIDE = False


def mx_kscale(k):
    if not WIDE:
        return np.ones(k)
    levels = np.array([10, -10, 5, -5, 0])
    if k % 512:
        return np.exp2(np.random.permutation(np.resize(levels, k // 32))).repeat(32)
    a = np.empty((k // 512, 16))
    for p in range(k // 512):
        a[p, :8] = np.random.permutation(np.resize(levels, 8))
        for g in range(8):
            far = levels[np.abs(levels - a[p, g]) >= 10]
            a[p, g + 8] = far[np.random.randint(len(far))]
    return np.exp2(a.ravel()).repeat(32)


def f64(x):
    return np.asarray(x).astype(np.float64)


def striped(idx):
    return np.tile(np.asarray(idx).reshape(-1, 16).T, (8, 1)).astype(np.uint16)


def unstriped(offs):
    return offs[:16].T.reshape(-1).astype(np.int64)


def striped8(idx):
    return np.asarray(idx).reshape(8, -1, 16).transpose(0, 2, 1).reshape(128, -1).astype(np.uint16)


def unstriped8(offs):
    return offs.reshape(8, 16, -1).transpose(0, 2, 1).reshape(8, -1).astype(np.int64)


def pick8(x, idx, run):
    r = np.arange(len(x))
    return x[r[:, None], idx[r % (8 * run) // run]]


E2M1 = np.array([0.0, 0.5, 1.0, 1.5, 2.0, 3.0, 4.0, 6.0, -0.0, -0.5, -1.0, -1.5, -2.0, -3.0, -4.0, -6.0])


def pack_weight(w, fmt):
    k, n = w.shape
    w = f64(np.asarray(w, np.float32).astype(ml_dtypes.bfloat16)).reshape(k // 32, 32, n)
    amax = np.abs(w).max(1)
    if fmt == "e4m3":
        byte = np.frexp(amax)[1] - 1 + 127 - 7
    else:
        mant, ex = np.frexp(amax / 6.0)
        byte = np.where(mant > 0.5, ex, ex - 1) + 127
    byte = np.clip(np.where(amax > 0, byte, 1), 1, 254)
    scaled = (w * np.exp2(127.0 - byte)[:, None, :]).reshape(k, n).astype(np.float32)
    by_word = np.ascontiguousarray(scaled.reshape(k // 512, 128, 4, n).transpose(0, 1, 3, 2))
    if fmt == "e4m3":
        words = by_word.astype(ml_dtypes.float8_e4m3fn).view(np.uint8)
    else:
        c = by_word.astype(ml_dtypes.float4_e2m1fn).view(np.uint8) & 0xF
        words = (c[..., 0::2] | (c[..., 1::2] << 4)).reshape(k // 512, 128, 2 * n)
    return np.ascontiguousarray(words), np.ascontiguousarray(byte.astype(np.uint8).reshape(k // 512, 16, n))


def unpack_weight(words, scales, fmt):
    g, _, n = scales.shape
    words = np.ascontiguousarray(words).reshape(g, 128, n, -1)
    if fmt == "e4m3":
        vals = words.view(ml_dtypes.float8_e4m3fn).astype(np.float64)
    else:
        nib = np.empty((g, 128, n, 4), np.uint8)
        nib[..., 0::2] = words & 0xF
        nib[..., 1::2] = words >> 4
        vals = E2M1[nib]
    vals = vals * np.repeat(np.exp2(scales.astype(np.float64) - 127.0), 8, axis=1)[..., None]
    return vals.transpose(0, 1, 3, 2).reshape(g * 512, n)


K, J, R, T, U, F, O, S, N, Z = 512, 512, 512, 1024, 1024, 1024, 128, 256, 256, 1024


def setup_inputs():
    n = np.random.standard_normal
    idx = np.stack([np.random.permutation(T)[:J] for _ in range(8)])
    idx2 = np.stack([np.random.permutation(U)[:J] for _ in range(8)])
    idx3 = np.stack([np.random.permutation(F)[:R] for _ in range(8)])
    idx4 = np.stack([np.random.permutation(J)[:S] for _ in range(8)])
    idx5 = np.stack([np.random.permutation(S)[:O] for _ in range(8)])
    idx6 = np.random.permutation(S)[:O]
    idx7 = np.random.permutation(Z)[:N]
    fk = mx_kscale(K)
    fr = mx_kscale(R)
    vsp = pack_weight(n((R, Z)) * 1 / np.sqrt(R) / fr[:, None], "e2m1")
    return {
        "ta": (np.random.randint(-7, 8, (K, T)).astype(np.float64)).astype(np.float32),
        "tb": (np.random.randint(-7, 8, (K, U)).astype(np.float64)).astype(np.float32),
        "ga": ((np.random.randint(8, 25, (K, 1)) / 64.0) * fk[:, None]).astype(np.float32),
        "gb": ((np.random.randint(8, 25, (K, 1)) / 64.0) * fk[:, None]).astype(np.float32),
        "ua": (np.random.randint(-7, 8, (K, F)).astype(np.float64)).astype(np.float32),
        "ha": ((np.random.randint(8, 25, (K, 1)) / 1024.0) / fk[:, None]).astype(np.float32),
        "sa": (np.random.uniform(0.5, 1.6, (R, 1)) * fr[:, None]).astype(np.float32),
        "sb": (np.random.uniform(0.5, 1.6, (R, 1))).astype(np.float32),
        "sd": (np.random.uniform(0.5, 1.6, (R, 1))).astype(np.float32),
        "vs_words": vsp[0],
        "vs_scales": vsp[1],
        "offs": striped8(idx),
        "offs2": striped8(idx2),
        "offs3": striped8(idx3),
        "offs4": striped8(idx4),
        "offs5": striped8(idx5),
        "offs6": striped(idx6),
        "offs7": striped(idx7),
    }


def reference(ta, tb, ga, gb, ua, ha, sa, sb, sd, vs_words, vs_scales, offs, offs2, offs3, offs4, offs5, offs6, offs7):
    idx = unstriped8(offs)
    idx2 = unstriped8(offs2)
    idx3 = unstriped8(offs3)
    idx4 = unstriped8(offs4)
    idx5 = unstriped8(offs5)
    idx6 = unstriped(offs6)
    idx7 = unstriped(offs7)
    vsu = unpack_weight(vs_words, vs_scales, "e2m1")
    xc = np.maximum(pick8(f64(ta), idx, 64) * f64(ga), pick8(f64(tb), idx2, 64) * f64(gb))
    wc = pick8(f64(ua), idx3, 64) * f64(ha)
    wcq = mxq(wc, 0, "e4m3")
    xcq = mxq(xc, 0, "e4m3")
    a = wcq.T @ xcq
    h1 = pick8(a, idx4, 64) * f64(sa)
    hid = np.abs(pick8(h1, idx5, 64) * f64(sb) - h1[:, idx6] * f64(sd))
    vsidx7g = vsu[:, idx7]
    hidq = mxq(hid, 0, "e4m3")
    y = vsidx7g.T @ hidq
    return y

@@ -1,0 +1,210 @@
+from contextlib import ExitStack
+
+import concourse.mybir as mybir
+
+K, J, R, T, O, S, N, Z = 512, 512, 512, 1024, 128, 256, 256, 1024
+FLOPS = 2 * K * R * J + 2 * R * N * O
+
+F32 = mybir.dt.float32
+BF16 = mybir.dt.bfloat16
+I32 = mybir.dt.int32
+U32 = mybir.dt.uint32
+U16 = mybir.dt.uint16
+U8 = mybir.dt.uint8
+FP8X4 = mybir.dt.float8_e4m3fn_x4
+FP4X4 = mybir.dt.float4_e2m1fn_x4
+ALU = mybir.AluOpType
+COPY = mybir.ActivationFunctionType.Copy
+
+P = 128
+PACK = 4
+HALF = J // 2
+
+
+def tile_picked_largercode_codes_one_chain_store_plain_kernel(
+    tc, ta, tb, ga, gb, ua, ha, sa, sb, sd, vs_words, vs_scales,
+    offs, offs2, offs3, offs4, offs5, offs6, offs7, out,
+):
+    nc = tc.nc
+    with ExitStack() as ctx:
+        keep = ctx.enter_context(tc.tile_pool(name="keep", bufs=1))
+        psum = ctx.enter_context(tc.psum_pool(name="psum", bufs=1))
+
+        def load_list(name, dram):
+            tile = keep.tile(list(dram.shape), U16, name=name)
+            nc.sync.dma_start(tile[:], dram)
+            return tile
+
+        def load_steps(name, dram, queue):
+            tile = keep.tile([P, PACK], F32, name=name)
+            queue.dma_start(out=tile[:], in_=dram.rearrange("(p t) o -> p (t o)", t=PACK))
+            return tile
+
+        def load_rows(name, dram, t):
+            tile = keep.tile([P, T], F32, name=name)
+            nc.sync.dma_start(out=tile[:], in_=dram.rearrange("(p t) c -> p t c", t=PACK)[:, t, :])
+            return tile
+
+        def fetch(dst, window, offsets, steps, t):
+            nc.scalar.activation(out=dst, in_=window[:].indirect(offsets), func=COPY, scale=steps[:, t : t + 1])
+
+        ga_t = load_steps("ga_t", ga, nc.scalar)
+        gb_t = load_steps("gb_t", gb, nc.scalar)
+        vs_w = keep.tile([P, Z], U16, name="vs_w")
+        vs_s = keep.tile([P, Z], U8, name="vs_s")
+        nc.vector.memset(vs_s[:].bitcast(I32), 0)
+
+        def load_scale_rows(q):
+            nc.sync.dma_start(
+                out=vs_s[32 * q : 32 * q + 4, :].bitcast(I32),
+                in_=vs_scales[0, 4 * q : 4 * q + 4, :].bitcast(I32),
+            )
+
+        ta_w = [load_rows("ta0", ta, 0)]
+        l1 = load_list("l1", offs)
+        tb_w = [load_rows("tb0", tb, 0)]
+        l2 = load_list("l2", offs2)
+        for t in range(1, PACK - 1):
+            ta_w.append(load_rows("ta%d" % t, ta, t))
+            load_scale_rows(2 * t - 2)
+            tb_w.append(load_rows("tb%d" % t, tb, t))
+            load_scale_rows(2 * t - 1)
+        ta_w.append(load_rows("ta3", ta, PACK - 1))
+        l7 = load_list("l7", offs7)
+        nc.sync.dma_start(out=vs_w[:].bitcast(I32), in_=vs_words[0].bitcast(I32))
+        tb_w.append(load_rows("tb3", tb, PACK - 1))
+        l3 = load_list("l3", offs3)
+        ha_t = load_steps("ha_t", ha, nc.sync)
+        ua_w = [load_rows("ua%d" % t, ua, t) for t in range(PACK)]
+        l4 = load_list("l4", offs4)
+        sa_t = load_steps("sa_t", sa, nc.sync)
+        l5 = load_list("l5", offs5)
+        sb_t = load_steps("sb_t", sb, nc.sync)
+        l6 = load_list("l6", offs6)
+        sd_t = load_steps("sd_t", sd, nc.sync)
+
+        x_bf = keep.tile([P, J, PACK], BF16, name="x_bf", align_bytes=64)
+        for pair in range(2):
+            pa = keep.tile([P, 2, J], F32, name="pa%d" % pair)
+            pb = keep.tile([P, 2, J], F32, name="pb%d" % pair)
+            for e in range(2):
+                t = 2 * pair + e
+                fetch(pa[:, e, :], ta_w[t], l1[:], ga_t, t)
+                fetch(pb[:, e, :], tb_w[t], l2[:], gb_t, t)
+            nc.vector.tensor_tensor(
+                out=x_bf[:, :, 2 * pair : 2 * pair + 2], in0=pa[:].rearrange("p e j -> p j e"),
+                in1=pb[:].rearrange("p e j -> p j e"), op=ALU.max,
+            )
+        x_codes = keep.tile([P, J], U32, name="x_codes", align_bytes=64)
+        x_scales = keep.tile([P, J], U8, name="x_scales", align_bytes=64)
+        nc.vector.quantize_mx(
+            out=x_codes[:].bitcast(FP8X4), scales=x_scales[:], in_=x_bf[:].rearrange("p j t -> p (j t)")
+        )
+
+        v_codes = keep.tile([P, N], U16, name="v_codes", align_bytes=64)
+        v_scales = keep.tile([P, N], U8, name="v_scales", align_bytes=64)
+        nc.vector.tensor_copy(out=v_codes[:], in_=vs_w[:].indirect(l7[:]))
+        nc.vector.tensor_copy(out=v_scales[:], in_=vs_s[:].indirect(l7[:]))
+
+        w_lo = keep.tile([P, 2, R], BF16, name="w_lo")
+        w_hi = keep.tile([P, 2, R], BF16, name="w_hi")
+        w_first = keep.tile([P, 1, P, PACK], BF16, name="w_first", align_bytes=64)
+        w_rest = keep.tile([P, PACK - 1, P, PACK], BF16, name="w_rest", align_bytes=64)
+        cols = R // 2 // 16
+
+        def deal(src, ms, ts):
+            view = src.rearrange("p e (m u) -> p u m e", u=PACK)
+            nc.vector.tensor_copy(out=w_first[:, :, ms, ts], in_=view[:, 0:1])
+            nc.vector.tensor_copy(out=w_rest[:, :, ms, ts], in_=view[:, 1:PACK])
+
+        for t in range(2):
+            fetch(w_lo[:, t, :], ua_w[t], l3[:], ha_t, t)
+        deal(w_lo[:], slice(0, P), slice(0, 2))
+        fetch(w_hi[:, 0, :], ua_w[2], l3[:], ha_t, 2)
+        for h in range(2):
+            rs = slice(h * R // 2, (h + 1) * R // 2)
+            fetch(w_hi[:, 1, rs], ua_w[3], l3[:, h * cols : (h + 1) * cols], ha_t, 3)
+            deal(w_hi[:, :, rs], slice(h * P // 2, (h + 1) * P // 2), slice(2, 4))
+        w_codes = [keep.tile([P, P], U32, name="w_codes0", align_bytes=64),
+                   keep.tile([P, (PACK - 1) * P], U32, name="w_codes1", align_bytes=64)]
+        w_scales = [keep.tile([P, P], U8, name="w_scales0", align_bytes=64),
+                    keep.tile([P, (PACK - 1) * P], U8, name="w_scales1", align_bytes=64)]
+        for i, src in enumerate((w_first, w_rest)):
+            nc.vector.quantize_mx(
+                out=w_codes[i][:].bitcast(FP8X4), scales=w_scales[i][:], in_=src[:].rearrange("p u m t -> p (u m t)")
+            )
+
+        a_w = [keep.tile([P, J], F32, name="a%d" % u) for u in range(PACK)]
+        for h in range(4):
+            js = slice(h * P, (h + 1) * P)
+            acc = psum.tile([P, P], F32, name="acc0_%d" % h, tag="bank%d" % h)
+            nc.tensor.matmul_mx(
+                out=acc[:], lhsT=w_codes[0][:].bitcast(FP8X4), lhsT_scale=w_scales[0][:],
+                rhs=x_codes[:, js].bitcast(FP8X4), rhs_scale=x_scales[:, js], start=True, stop=True,
+            )
+            if h != 1:
+                nc.scalar.copy(out=a_w[0][:, js], in_=acc[:])
+            else:
+                nc.vector.tensor_copy(out=a_w[0][:, js], in_=acc[:])
+        for u in range(1, PACK):
+            acc = psum.tile([P, J], F32, name="acc%d" % u)
+            ms = slice((u - 1) * P, u * P)
+            nc.tensor.matmul_mx(
+                out=acc[:], lhsT=w_codes[1][:, ms].bitcast(FP8X4), lhsT_scale=w_scales[1][:, ms],
+                rhs=x_codes[:].bitcast(FP8X4), rhs_scale=x_scales[:], start=True, stop=True,
+            )
+            nc.vector.tensor_copy(out=a_w[u][:], in_=acc[:])
+
+        hid_bf = keep.tile([P, O, PACK], BF16, name="hid_bf", align_bytes=64)
+        h1 = [keep.tile([P, S], F32, name="h1_%d" % u) for u in range(PACK)]
+        diff = [keep.tile([P, 2, O], F32, name="diff%d" % pair) for pair in range(2)]
+
+        def second_lookup(u):
+            pair, e = divmod(u, 2)
+            hb = keep.tile([P, O], F32, name="hb%d" % u)
+            hd = keep.tile([P, O], F32, name="hd%d" % u)
+            pieces = 2 if u == PACK - 1 else 1
+            width = O // pieces
+            for c in range(pieces):
+                places = slice(c * width, (c + 1) * width)
+                entries = slice(c * width // 16, (c + 1) * width // 16)
+                fetch(hb[:, places], h1[u], l5[:, entries], sb_t, u)
+                fetch(hd[:, places], h1[u], l6[:, entries], sd_t, u)
+                nc.vector.tensor_tensor(
+                    out=diff[pair][:, e, places], in0=hb[:, places], in1=hd[:, places], op=ALU.subtract
+                )
+                if e == 1:
+                    both = diff[pair][:, :, places].rearrange("p e o -> p o e")
+                    nc.vector.scalar_tensor_tensor(
+                        out=hid_bf[:, places, 2 * pair : 2 * pair + 2], in0=both, scalar=-1.0, in1=both,
+                        op0=ALU.mult, op1=ALU.max,
+                    )
+
+        for u in range(PACK):
+            fetch(h1[u][:], a_w[u], l4[:], sa_t, u)
+            if u > 0:
+                second_lookup(u - 1)
+        second_lookup(PACK - 1)
+
+        h_codes = keep.tile([P, O], U32, name="h_codes", align_bytes=64)
+        h_scales = keep.tile([P, O], U8, name="h_scales", align_bytes=64)
+        for c in range(2):
+            places = slice(c * O // 2, (c + 1) * O // 2)
+            nc.vector.quantize_mx(
+                out=h_codes[:, places].bitcast(FP8X4), scales=h_scales[:, places],
+                in_=hid_bf[:, places, :].rearrange("p o u -> p (o u)"),
+            )
+        for b in range(N // P):
+            ns = slice(b * P, (b + 1) * P)
+            acc = psum.tile([P, O], F32, name="y%d" % b, tag="bank%d" % b)
+            nc.tensor.matmul_mx(
+                out=acc[:], lhsT=v_codes[:, ns].bitcast(FP4X4), lhsT_scale=v_scales[:, ns],
+                rhs=h_codes[:].bitcast(FP8X4), rhs_scale=h_scales[:], start=True, stop=True,
+            )
+            res = keep.tile([P, O], F32, name="res%d" % b)
+            if b == 0:
+                nc.vector.tensor_copy(out=res[:], in_=acc[:])
+                nc.sync.dma_start(out=out[ns, :], in_=res[:])
+            else:
+                nc.scalar.copy(out=res[:], in_=acc[:])
+                nc.scalar.dma_start(out=out[ns, :], in_=res[:])

@@ -50,6 +50,10 @@ def tile_picked_largercode_codes_one_chain_store_plain_kernel(
 
         ga_t = load_steps("ga_t", ga, nc.scalar)
         gb_t = load_steps("gb_t", gb, nc.scalar)
+        warm_in = keep.tile([P, 1], F32, name="warm_in")
+        warm_out = keep.tile([P, 1], F32, name="warm_out")
+        nc.vector.memset(warm_in[:], 0.0)
+        nc.scalar.activation(out=warm_out[:], in_=warm_in[:], func=COPY)
         vs_w = keep.tile([P, Z], U16, name="vs_w")
         vs_s = keep.tile([P, Z], U8, name="vs_s")
         nc.vector.memset(vs_s[:].bitcast(I32), 0)

@@ -15,6 +15,7 @@ FP8X4 = mybir.dt.float8_e4m3fn_x4
 FP4X4 = mybir.dt.float4_e2m1fn_x4
 ALU = mybir.AluOpType
 COPY = mybir.ActivationFunctionType.Copy
+ABS = mybir.ActivationFunctionType.Abs
 
 P = 128
 PACK = 4
@@ -54,32 +55,26 @@ def tile_picked_largercode_codes_one_chain_store_plain_kernel(
         warm_out = keep.tile([P, 1], F32, name="warm_out")
         nc.vector.memset(warm_in[:], 0.0)
         nc.scalar.activation(out=warm_out[:], in_=warm_in[:], func=COPY)
-        vs_w = keep.tile([P, Z], U16, name="vs_w")
-        vs_s = keep.tile([P, Z], U8, name="vs_s")
-        nc.vector.memset(vs_s[:].bitcast(I32), 0)
-
-        def load_scale_rows(q):
-            nc.sync.dma_start(
-                out=vs_s[32 * q : 32 * q + 4, :].bitcast(I32),
-                in_=vs_scales[0, 4 * q : 4 * q + 4, :].bitcast(I32),
-            )
-
+        ha_t = load_steps("ha_t", ha, nc.gpsimd)
         ta_w = [load_rows("ta0", ta, 0)]
         l1 = load_list("l1", offs)
         tb_w = [load_rows("tb0", tb, 0)]
         l2 = load_list("l2", offs2)
-        for t in range(1, PACK - 1):
+        for t in range(1, PACK):
             ta_w.append(load_rows("ta%d" % t, ta, t))
-            load_scale_rows(2 * t - 2)
             tb_w.append(load_rows("tb%d" % t, tb, t))
-            load_scale_rows(2 * t - 1)
-        ta_w.append(load_rows("ta3", ta, PACK - 1))
-        l7 = load_list("l7", offs7)
-        nc.sync.dma_start(out=vs_w[:].bitcast(I32), in_=vs_words[0].bitcast(I32))
-        tb_w.append(load_rows("tb3", tb, PACK - 1))
         l3 = load_list("l3", offs3)
-        ha_t = load_steps("ha_t", ha, nc.sync)
         ua_w = [load_rows("ua%d" % t, ua, t) for t in range(PACK)]
+        l7 = load_list("l7", offs7)
+        vs_w = keep.tile([P, Z], U16, name="vs_w")
+        nc.sync.dma_start(out=vs_w[:].bitcast(I32), in_=vs_words[0].bitcast(I32))
+        vs_s = keep.tile([P, Z], U8, name="vs_s")
+        nc.vector.memset(vs_s[:].bitcast(I32), 0)
+        for q in range(4):
+            nc.sync.dma_start(
+                out=vs_s[32 * q : 32 * q + 4, :].bitcast(I32),
+                in_=vs_scales[0, 4 * q : 4 * q + 4, :].bitcast(I32),
+            )
         l4 = load_list("l4", offs4)
         sa_t = load_steps("sa_t", sa, nc.sync)
         l5 = load_list("l5", offs5)
@@ -100,15 +95,10 @@ def tile_picked_largercode_codes_one_chain_store_plain_kernel(
                 in1=pb[:].rearrange("p e j -> p j e"), op=ALU.max,
             )
         x_codes = keep.tile([P, J], U32, name="x_codes", align_bytes=64)
-        x_scales = keep.tile([P, J], U8, name="x_scales", align_bytes=64)
+        x_scales = keep.tile([P, J], U8, name="x_scales", tag="held_c", align_bytes=64)
         nc.vector.quantize_mx(
             out=x_codes[:].bitcast(FP8X4), scales=x_scales[:], in_=x_bf[:].rearrange("p j t -> p (j t)")
         )
-
-        v_codes = keep.tile([P, N], U16, name="v_codes", align_bytes=64)
-        v_scales = keep.tile([P, N], U8, name="v_scales", align_bytes=64)
-        nc.vector.tensor_copy(out=v_codes[:], in_=vs_w[:].indirect(l7[:]))
-        nc.vector.tensor_copy(out=v_scales[:], in_=vs_s[:].indirect(l7[:]))
 
         w_lo = keep.tile([P, 2, R], BF16, name="w_lo")
         w_hi = keep.tile([P, 2, R], BF16, name="w_hi")
@@ -125,18 +115,22 @@ def tile_picked_largercode_codes_one_chain_store_plain_kernel(
             fetch(w_lo[:, t, :], ua_w[t], l3[:], ha_t, t)
         deal(w_lo[:], slice(0, P), slice(0, 2))
         fetch(w_hi[:, 0, :], ua_w[2], l3[:], ha_t, 2)
-        for h in range(2):
-            rs = slice(h * R // 2, (h + 1) * R // 2)
-            fetch(w_hi[:, 1, rs], ua_w[3], l3[:, h * cols : (h + 1) * cols], ha_t, 3)
-            deal(w_hi[:, :, rs], slice(h * P // 2, (h + 1) * P // 2), slice(2, 4))
         w_codes = [keep.tile([P, P], U32, name="w_codes0", align_bytes=64),
                    keep.tile([P, (PACK - 1) * P], U32, name="w_codes1", align_bytes=64)]
         w_scales = [keep.tile([P, P], U8, name="w_scales0", align_bytes=64),
-                    keep.tile([P, (PACK - 1) * P], U8, name="w_scales1", align_bytes=64)]
-        for i, src in enumerate((w_first, w_rest)):
+                    keep.tile([P, (PACK - 1) * P], U8, name="w_scales1", tag="held_s", align_bytes=64)]
+        for h in range(2):
+            rs = slice(h * R // 2, (h + 1) * R // 2)
+            ms = slice(h * P // 2, (h + 1) * P // 2)
+            fetch(w_hi[:, 1, rs], ua_w[3], l3[:, h * cols : (h + 1) * cols], ha_t, 3)
+            deal(w_hi[:, :, rs], ms, slice(2, 4))
             nc.vector.quantize_mx(
-                out=w_codes[i][:].bitcast(FP8X4), scales=w_scales[i][:], in_=src[:].rearrange("p u m t -> p (u m t)")
+                out=w_codes[0][:, ms].bitcast(FP8X4), scales=w_scales[0][:, ms],
+                in_=w_first[:, 0, ms, :].rearrange("p m t -> p (m t)"),
             )
+        nc.vector.quantize_mx(
+            out=w_codes[1][:].bitcast(FP8X4), scales=w_scales[1][:], in_=w_rest[:].rearrange("p u m t -> p (u m t)")
+        )
 
         a_w = [keep.tile([P, J], F32, name="a%d" % u) for u in range(PACK)]
         for h in range(4):
@@ -146,18 +140,27 @@ def tile_picked_largercode_codes_one_chain_store_plain_kernel(
                 out=acc[:], lhsT=w_codes[0][:].bitcast(FP8X4), lhsT_scale=w_scales[0][:],
                 rhs=x_codes[:, js].bitcast(FP8X4), rhs_scale=x_scales[:, js], start=True, stop=True,
             )
-            if h != 1:
+            if h < 2:
                 nc.scalar.copy(out=a_w[0][:, js], in_=acc[:])
             else:
                 nc.vector.tensor_copy(out=a_w[0][:, js], in_=acc[:])
         for u in range(1, PACK):
-            acc = psum.tile([P, J], F32, name="acc%d" % u)
             ms = slice((u - 1) * P, u * P)
-            nc.tensor.matmul_mx(
-                out=acc[:], lhsT=w_codes[1][:, ms].bitcast(FP8X4), lhsT_scale=w_scales[1][:, ms],
-                rhs=x_codes[:].bitcast(FP8X4), rhs_scale=x_scales[:], start=True, stop=True,
-            )
-            nc.vector.tensor_copy(out=a_w[u][:], in_=acc[:])
+            pieces = 2 if u == 1 else 1
+            width = J // pieces
+            for c in range(pieces):
+                js = slice(c * width, (c + 1) * width)
+                acc = psum.tile([P, width], F32, name="acc%d_%d" % (u, c))
+                nc.tensor.matmul_mx(
+                    out=acc[:], lhsT=w_codes[1][:, ms].bitcast(FP8X4), lhsT_scale=w_scales[1][:, ms],
+                    rhs=x_codes[:, js].bitcast(FP8X4), rhs_scale=x_scales[:, js], start=True, stop=True,
+                )
+                nc.vector.tensor_copy(out=a_w[u][:, js], in_=acc[:])
+
+        v_codes = keep.tile([P, N], U16, name="v_codes", tag="held_c", align_bytes=64)
+        v_scales = keep.tile([P, N], U8, name="v_scales", tag="held_s", align_bytes=64)
+        nc.vector.tensor_copy(out=v_codes[:], in_=vs_w[:].indirect(l7[:]))
+        nc.vector.tensor_copy(out=v_scales[:], in_=vs_s[:].indirect(l7[:]))
 
         hid_bf = keep.tile([P, O, PACK], BF16, name="hid_bf", align_bytes=64)
         h1 = [keep.tile([P, S], F32, name="h1_%d" % u) for u in range(PACK)]
@@ -179,10 +182,13 @@ def tile_picked_largercode_codes_one_chain_store_plain_kernel(
                 )
                 if e == 1:
                     both = diff[pair][:, :, places].rearrange("p e o -> p o e")
-                    nc.vector.scalar_tensor_tensor(
-                        out=hid_bf[:, places, 2 * pair : 2 * pair + 2], in0=both, scalar=-1.0, in1=both,
-                        op0=ALU.mult, op1=ALU.max,
-                    )
+                    dst = hid_bf[:, places, 2 * pair : 2 * pair + 2]
+                    if u == PACK - 1 and c == pieces - 1:
+                        nc.scalar.activation(out=dst, in_=both, func=ABS)
+                    else:
+                        nc.vector.scalar_tensor_tensor(
+                            out=dst, in0=both, scalar=-1.0, in1=both, op0=ALU.mult, op1=ALU.max
+                        )
 
         for u in range(PACK):
             fetch(h1[u][:], a_w[u], l4[:], sa_t, u)

@@ -55,7 +55,7 @@ def tile_picked_largercode_codes_one_chain_store_plain_kernel(
         warm_out = keep.tile([P, 1], F32, name="warm_out")
         nc.vector.memset(warm_in[:], 0.0)
         nc.scalar.activation(out=warm_out[:], in_=warm_in[:], func=COPY)
-        ha_t = load_steps("ha_t", ha, nc.gpsimd)
+        ha_t = load_steps("ha_t", ha, nc.scalar)
         ta_w = [load_rows("ta0", ta, 0)]
         l1 = load_list("l1", offs)
         tb_w = [load_rows("tb0", tb, 0)]
@@ -64,6 +64,8 @@ def tile_picked_largercode_codes_one_chain_store_plain_kernel(
             ta_w.append(load_rows("ta%d" % t, ta, t))
             tb_w.append(load_rows("tb%d" % t, tb, t))
         l3 = load_list("l3", offs3)
+        l5 = load_list("l5", offs5)
+        l6 = load_list("l6", offs6)
         ua_w = [load_rows("ua%d" % t, ua, t) for t in range(PACK)]
         l7 = load_list("l7", offs7)
         vs_w = keep.tile([P, Z], U16, name="vs_w")
@@ -77,88 +79,90 @@ def tile_picked_largercode_codes_one_chain_store_plain_kernel(
             )
         l4 = load_list("l4", offs4)
         sa_t = load_steps("sa_t", sa, nc.sync)
-        l5 = load_list("l5", offs5)
         sb_t = load_steps("sb_t", sb, nc.sync)
-        l6 = load_list("l6", offs6)
         sd_t = load_steps("sd_t", sd, nc.sync)
 
         x_bf = keep.tile([P, J, PACK], BF16, name="x_bf", align_bytes=64)
-        for pair in range(2):
-            pa = keep.tile([P, 2, J], F32, name="pa%d" % pair)
-            pb = keep.tile([P, 2, J], F32, name="pb%d" % pair)
-            for e in range(2):
-                t = 2 * pair + e
-                fetch(pa[:, e, :], ta_w[t], l1[:], ga_t, t)
-                fetch(pb[:, e, :], tb_w[t], l2[:], gb_t, t)
-            nc.vector.tensor_tensor(
-                out=x_bf[:, :, 2 * pair : 2 * pair + 2], in0=pa[:].rearrange("p e j -> p j e"),
-                in1=pb[:].rearrange("p e j -> p j e"), op=ALU.max,
-            )
+        x_rows = keep.tile([P, PACK, J], BF16, name="x_rows")
+        for t in range(PACK):
+            pa = keep.tile([P, J], F32, name="pa%d" % t)
+            pb = keep.tile([P, J], F32, name="pb%d" % t)
+            fetch(pa[:], ta_w[t], l1[:], ga_t, t)
+            fetch(pb[:], tb_w[t], l2[:], gb_t, t)
+            nc.vector.tensor_tensor(out=x_rows[:, t, :], in0=pa[:], in1=pb[:], op=ALU.max)
+        nc.vector.tensor_copy(
+            out=x_bf[:].rearrange("p (c i) t -> p c t i", i=4),
+            in_=x_rows[:].rearrange("p t (c i) -> p c t i", i=4),
+        )
         x_codes = keep.tile([P, J], U32, name="x_codes", align_bytes=64)
         x_scales = keep.tile([P, J], U8, name="x_scales", tag="held_c", align_bytes=64)
         nc.vector.quantize_mx(
             out=x_codes[:].bitcast(FP8X4), scales=x_scales[:], in_=x_bf[:].rearrange("p j t -> p (j t)")
         )
 
-        w_lo = keep.tile([P, 2, R], BF16, name="w_lo")
-        w_hi = keep.tile([P, 2, R], BF16, name="w_hi")
-        w_first = keep.tile([P, 1, P, PACK], BF16, name="w_first", align_bytes=64)
-        w_rest = keep.tile([P, PACK - 1, P, PACK], BF16, name="w_rest", align_bytes=64)
+        w_rows = keep.tile([P, PACK, R], BF16, name="w_rows")
+        groups = ((0, 1), (1, 2), (2, 4))
+        w_bf = [keep.tile([P, hi - lo, P, PACK], BF16, name="w_bf%d" % lo, align_bytes=64) for lo, hi in groups]
+        w_codes = [keep.tile([P, (hi - lo) * P], U32, name="w_codes%d" % lo, align_bytes=64) for lo, hi in groups]
+        w_scales = [
+            keep.tile([P, (hi - lo) * P], U8, name="w_scales%d" % lo, tag="w_scales%d" % lo, align_bytes=64)
+            for lo, hi in groups
+        ]
         cols = R // 2 // 16
+        for t in range(PACK - 1):
+            fetch(w_rows[:, t, :], ua_w[t], l3[:], ha_t, t)
 
-        def deal(src, ms, ts):
-            view = src.rearrange("p e (m u) -> p u m e", u=PACK)
-            nc.vector.tensor_copy(out=w_first[:, :, ms, ts], in_=view[:, 0:1])
-            nc.vector.tensor_copy(out=w_rest[:, :, ms, ts], in_=view[:, 1:PACK])
+        def deal(g, h):
+            lo, hi = groups[g]
+            view = w_rows[:, :, h * R // 2 : (h + 1) * R // 2].rearrange("p t (m u) -> p m t u", u=PACK)
+            nc.vector.tensor_copy(
+                out=w_bf[g][:, :, h * P // 2 : (h + 1) * P // 2, :].rearrange("p u m t -> p m t u"),
+                in_=view[:, :, :, lo:hi],
+            )
 
-        for t in range(2):
-            fetch(w_lo[:, t, :], ua_w[t], l3[:], ha_t, t)
-        deal(w_lo[:], slice(0, P), slice(0, 2))
-        fetch(w_hi[:, 0, :], ua_w[2], l3[:], ha_t, 2)
-        w_codes = [keep.tile([P, P], U32, name="w_codes0", align_bytes=64),
-                   keep.tile([P, (PACK - 1) * P], U32, name="w_codes1", align_bytes=64)]
-        w_scales = [keep.tile([P, P], U8, name="w_scales0", align_bytes=64),
-                    keep.tile([P, (PACK - 1) * P], U8, name="w_scales1", tag="held_s", align_bytes=64)]
+        def quantise_w(g, ms):
+            flat = w_bf[g][:].rearrange("p u m t -> p (u m) t")
+            nc.vector.quantize_mx(
+                out=w_codes[g][:, ms].bitcast(FP8X4), scales=w_scales[g][:, ms],
+                in_=flat[:, ms, :].rearrange("p m t -> p (m t)"),
+            )
+
         for h in range(2):
             rs = slice(h * R // 2, (h + 1) * R // 2)
-            ms = slice(h * P // 2, (h + 1) * P // 2)
-            fetch(w_hi[:, 1, rs], ua_w[3], l3[:, h * cols : (h + 1) * cols], ha_t, 3)
-            deal(w_hi[:, :, rs], ms, slice(2, 4))
-            nc.vector.quantize_mx(
-                out=w_codes[0][:, ms].bitcast(FP8X4), scales=w_scales[0][:, ms],
-                in_=w_first[:, 0, ms, :].rearrange("p m t -> p (m t)"),
-            )
-        nc.vector.quantize_mx(
-            out=w_codes[1][:].bitcast(FP8X4), scales=w_scales[1][:], in_=w_rest[:].rearrange("p u m t -> p (u m t)")
-        )
+            fetch(w_rows[:, PACK - 1, rs], ua_w[3], l3[:, h * cols : (h + 1) * cols], ha_t, PACK - 1)
+            deal(0, h)
+            deal(1, h)
+            quantise_w(0, slice(h * P // 2, (h + 1) * P // 2))
+            if h == 1:
+                quantise_w(1, slice(0, P))
+            deal(2, h)
 
         a_w = [keep.tile([P, J], F32, name="a%d" % u) for u in range(PACK)]
-        for h in range(4):
-            js = slice(h * P, (h + 1) * P)
-            acc = psum.tile([P, P], F32, name="acc0_%d" % h, tag="bank%d" % h)
-            nc.tensor.matmul_mx(
-                out=acc[:], lhsT=w_codes[0][:].bitcast(FP8X4), lhsT_scale=w_scales[0][:],
-                rhs=x_codes[:, js].bitcast(FP8X4), rhs_scale=x_scales[:, js], start=True, stop=True,
-            )
-            if h < 2:
-                nc.scalar.copy(out=a_w[0][:, js], in_=acc[:])
-            else:
-                nc.vector.tensor_copy(out=a_w[0][:, js], in_=acc[:])
-        for u in range(1, PACK):
-            ms = slice((u - 1) * P, u * P)
-            pieces = 2 if u == 1 else 1
+
+        def product(u, pieces, by_scalar):
+            g = min(u, 2)
+            ms = slice((u - groups[g][0]) * P, (u - groups[g][0] + 1) * P)
             width = J // pieces
             for c in range(pieces):
                 js = slice(c * width, (c + 1) * width)
-                acc = psum.tile([P, width], F32, name="acc%d_%d" % (u, c))
+                acc = psum.tile([P, width], F32, name="acc%d_%d" % (u, c), tag="bank%d_%d" % (u, c))
                 nc.tensor.matmul_mx(
-                    out=acc[:], lhsT=w_codes[1][:, ms].bitcast(FP8X4), lhsT_scale=w_scales[1][:, ms],
+                    out=acc[:], lhsT=w_codes[g][:, ms].bitcast(FP8X4), lhsT_scale=w_scales[g][:, ms],
                     rhs=x_codes[:, js].bitcast(FP8X4), rhs_scale=x_scales[:, js], start=True, stop=True,
                 )
-                nc.vector.tensor_copy(out=a_w[u][:, js], in_=acc[:])
+                if c < by_scalar:
+                    nc.scalar.copy(out=a_w[u][:, js], in_=acc[:])
+                else:
+                    nc.vector.tensor_copy(out=a_w[u][:, js], in_=acc[:])
+
+        product(0, 4, 3)
+        quantise_w(2, slice(0, 2 * P))
+        product(1, 2, 0)
+        product(2, 1, 0)
+        product(3, 1, 0)
 
         v_codes = keep.tile([P, N], U16, name="v_codes", tag="held_c", align_bytes=64)
-        v_scales = keep.tile([P, N], U8, name="v_scales", tag="held_s", align_bytes=64)
+        v_scales = keep.tile([P, N], U8, name="v_scales", tag="w_scales2", align_bytes=64)
         nc.vector.tensor_copy(out=v_codes[:], in_=vs_w[:].indirect(l7[:]))
         nc.vector.tensor_copy(out=v_scales[:], in_=vs_s[:].indirect(l7[:]))
 
@@ -206,7 +210,7 @@ def tile_picked_largercode_codes_one_chain_store_plain_kernel(
             )
         for b in range(N // P):
             ns = slice(b * P, (b + 1) * P)
-            acc = psum.tile([P, O], F32, name="y%d" % b, tag="bank%d" % b)
+            acc = psum.tile([P, O], F32, name="y%d" % b, tag="bank0_%d" % b)
             nc.tensor.matmul_mx(
                 out=acc[:], lhsT=v_codes[:, ns].bitcast(FP4X4), lhsT_scale=v_scales[:, ns],
                 rhs=h_codes[:].bitcast(FP8X4), rhs_scale=h_scales[:], start=True, stop=True,

from contextlib import ExitStack

import concourse.mybir as mybir

K, J, R, T, O, S, N, Z = 512, 512, 512, 1024, 128, 256, 256, 1024
FLOPS = 2 * K * R * J + 2 * R * N * O

F32 = mybir.dt.float32
BF16 = mybir.dt.bfloat16
I32 = mybir.dt.int32
U32 = mybir.dt.uint32
U16 = mybir.dt.uint16
U8 = mybir.dt.uint8
FP8X4 = mybir.dt.float8_e4m3fn_x4
FP4X4 = mybir.dt.float4_e2m1fn_x4
ALU = mybir.AluOpType
COPY = mybir.ActivationFunctionType.Copy
ABS = mybir.ActivationFunctionType.Abs

P = 128
PACK = 4
HALF = J // 2


def tile_picked_largercode_codes_one_chain_store_plain_kernel(
    tc, ta, tb, ga, gb, ua, ha, sa, sb, sd, vs_words, vs_scales,
    offs, offs2, offs3, offs4, offs5, offs6, offs7, out,
):
    nc = tc.nc
    with ExitStack() as ctx:
        keep = ctx.enter_context(tc.tile_pool(name="keep", bufs=1))
        psum = ctx.enter_context(tc.psum_pool(name="psum", bufs=1))

        def load_list(name, dram):
            tile = keep.tile(list(dram.shape), U16, name=name)
            nc.sync.dma_start(tile[:], dram)
            return tile

        def load_steps(name, dram, queue):
            tile = keep.tile([P, PACK], F32, name=name)
            queue.dma_start(out=tile[:], in_=dram.rearrange("(p t) o -> p (t o)", t=PACK))
            return tile

        def load_rows(name, dram, t):
            tile = keep.tile([P, T], F32, name=name)
            nc.sync.dma_start(out=tile[:], in_=dram.rearrange("(p t) c -> p t c", t=PACK)[:, t, :])
            return tile

        def fetch(dst, window, offsets, steps, t):
            nc.scalar.activation(out=dst, in_=window[:].indirect(offsets), func=COPY, scale=steps[:, t : t + 1])

        ga_t = load_steps("ga_t", ga, nc.scalar)
        gb_t = load_steps("gb_t", gb, nc.scalar)
        warm_in = keep.tile([P, 1], F32, name="warm_in")
        warm_out = keep.tile([P, 1], F32, name="warm_out")
        nc.vector.memset(warm_in[:], 0.0)
        nc.scalar.activation(out=warm_out[:], in_=warm_in[:], func=COPY)
        ha_t = load_steps("ha_t", ha, nc.scalar)
        ta_w = [load_rows("ta0", ta, 0)]
        l1 = load_list("l1", offs)
        tb_w = [load_rows("tb0", tb, 0)]
        l2 = load_list("l2", offs2)
        for t in range(1, PACK):
            ta_w.append(load_rows("ta%d" % t, ta, t))
            tb_w.append(load_rows("tb%d" % t, tb, t))
        l3 = load_list("l3", offs3)
        l5 = load_list("l5", offs5)
        l6 = load_list("l6", offs6)
        ua_w = [load_rows("ua%d" % t, ua, t) for t in range(PACK)]
        l7 = load_list("l7", offs7)
        vs_w = keep.tile([P, Z], U16, name="vs_w")
        nc.sync.dma_start(out=vs_w[:].bitcast(I32), in_=vs_words[0].bitcast(I32))
        vs_s = keep.tile([P, Z], U8, name="vs_s")
        nc.vector.memset(vs_s[:].bitcast(I32), 0)
        for q in range(4):
            nc.sync.dma_start(
                out=vs_s[32 * q : 32 * q + 4, :].bitcast(I32),
                in_=vs_scales[0, 4 * q : 4 * q + 4, :].bitcast(I32),
            )
        l4 = load_list("l4", offs4)
        sa_t = load_steps("sa_t", sa, nc.sync)
        sb_t = load_steps("sb_t", sb, nc.sync)
        sd_t = load_steps("sd_t", sd, nc.sync)

        x_bf = keep.tile([P, J, PACK], BF16, name="x_bf", align_bytes=64)
        x_rows = keep.tile([P, PACK, J], BF16, name="x_rows")
        for t in range(PACK):
            pa = keep.tile([P, J], F32, name="pa%d" % t)
            pb = keep.tile([P, J], F32, name="pb%d" % t)
            fetch(pa[:], ta_w[t], l1[:], ga_t, t)
            fetch(pb[:], tb_w[t], l2[:], gb_t, t)
            nc.vector.tensor_tensor(out=x_rows[:, t, :], in0=pa[:], in1=pb[:], op=ALU.max)
        nc.vector.tensor_copy(
            out=x_bf[:].rearrange("p (c i) t -> p c t i", i=4),
            in_=x_rows[:].rearrange("p t (c i) -> p c t i", i=4),
        )
        x_codes = keep.tile([P, J], U32, name="x_codes", align_bytes=64)
        x_scales = keep.tile([P, J], U8, name="x_scales", tag="held_c", align_bytes=64)
        nc.vector.quantize_mx(
            out=x_codes[:].bitcast(FP8X4), scales=x_scales[:], in_=x_bf[:].rearrange("p j t -> p (j t)")
        )

        w_rows = keep.tile([P, PACK, R], BF16, name="w_rows")
        groups = ((0, 1), (1, 2), (2, 4))
        w_bf = [keep.tile([P, hi - lo, P, PACK], BF16, name="w_bf%d" % lo, align_bytes=64) for lo, hi in groups]
        w_codes = [keep.tile([P, (hi - lo) * P], U32, name="w_codes%d" % lo, align_bytes=64) for lo, hi in groups]
        w_scales = [
            keep.tile([P, (hi - lo) * P], U8, name="w_scales%d" % lo, tag="w_scales%d" % lo, align_bytes=64)
            for lo, hi in groups
        ]
        cols = R // 2 // 16
        for t in range(PACK - 1):
            fetch(w_rows[:, t, :], ua_w[t], l3[:], ha_t, t)

        def deal(g, h):
            lo, hi = groups[g]
            view = w_rows[:, :, h * R // 2 : (h + 1) * R // 2].rearrange("p t (m u) -> p m t u", u=PACK)
            nc.vector.tensor_copy(
                out=w_bf[g][:, :, h * P // 2 : (h + 1) * P // 2, :].rearrange("p u m t -> p m t u"),
                in_=view[:, :, :, lo:hi],
            )

        def quantise_w(g, ms):
            flat = w_bf[g][:].rearrange("p u m t -> p (u m) t")
            nc.vector.quantize_mx(
                out=w_codes[g][:, ms].bitcast(FP8X4), scales=w_scales[g][:, ms],
                in_=flat[:, ms, :].rearrange("p m t -> p (m t)"),
            )

        for h in range(2):
            rs = slice(h * R // 2, (h + 1) * R // 2)
            fetch(w_rows[:, PACK - 1, rs], ua_w[3], l3[:, h * cols : (h + 1) * cols], ha_t, PACK - 1)
            deal(0, h)
            deal(1, h)
            quantise_w(0, slice(h * P // 2, (h + 1) * P // 2))
            if h == 1:
                quantise_w(1, slice(0, P))
            deal(2, h)

        a_w = [keep.tile([P, J], F32, name="a%d" % u) for u in range(PACK)]

        def product(u, pieces, by_scalar):
            g = min(u, 2)
            ms = slice((u - groups[g][0]) * P, (u - groups[g][0] + 1) * P)
            width = J // pieces
            for c in range(pieces):
                js = slice(c * width, (c + 1) * width)
                acc = psum.tile([P, width], F32, name="acc%d_%d" % (u, c), tag="bank%d_%d" % (u, c))
                nc.tensor.matmul_mx(
                    out=acc[:], lhsT=w_codes[g][:, ms].bitcast(FP8X4), lhsT_scale=w_scales[g][:, ms],
                    rhs=x_codes[:, js].bitcast(FP8X4), rhs_scale=x_scales[:, js], start=True, stop=True,
                )
                if c < by_scalar:
                    nc.scalar.copy(out=a_w[u][:, js], in_=acc[:])
                else:
                    nc.vector.tensor_copy(out=a_w[u][:, js], in_=acc[:])

        product(0, 4, 3)
        quantise_w(2, slice(0, 2 * P))
        product(1, 2, 0)
        product(2, 1, 0)
        product(3, 1, 0)

        v_codes = keep.tile([P, N], U16, name="v_codes", tag="held_c", align_bytes=64)
        v_scales = keep.tile([P, N], U8, name="v_scales", tag="w_scales2", align_bytes=64)
        nc.vector.tensor_copy(out=v_codes[:], in_=vs_w[:].indirect(l7[:]))
        nc.vector.tensor_copy(out=v_scales[:], in_=vs_s[:].indirect(l7[:]))

        hid_bf = keep.tile([P, O, PACK], BF16, name="hid_bf", align_bytes=64)
        h1 = [keep.tile([P, S], F32, name="h1_%d" % u) for u in range(PACK)]
        diff = [keep.tile([P, 2, O], F32, name="diff%d" % pair) for pair in range(2)]

        def second_lookup(u):
            pair, e = divmod(u, 2)
            hb = keep.tile([P, O], F32, name="hb%d" % u)
            hd = keep.tile([P, O], F32, name="hd%d" % u)
            pieces = 2 if u == PACK - 1 else 1
            width = O // pieces
            for c in range(pieces):
                places = slice(c * width, (c + 1) * width)
                entries = slice(c * width // 16, (c + 1) * width // 16)
                fetch(hb[:, places], h1[u], l5[:, entries], sb_t, u)
                fetch(hd[:, places], h1[u], l6[:, entries], sd_t, u)
                nc.vector.tensor_tensor(
                    out=diff[pair][:, e, places], in0=hb[:, places], in1=hd[:, places], op=ALU.subtract
                )
                if e == 1:
                    both = diff[pair][:, :, places].rearrange("p e o -> p o e")
                    dst = hid_bf[:, places, 2 * pair : 2 * pair + 2]
                    if u == PACK - 1 and c == pieces - 1:
                        nc.scalar.activation(out=dst, in_=both, func=ABS)
                    else:
                        nc.vector.scalar_tensor_tensor(
                            out=dst, in0=both, scalar=-1.0, in1=both, op0=ALU.mult, op1=ALU.max
                        )

        for u in range(PACK):
            fetch(h1[u][:], a_w[u], l4[:], sa_t, u)
            if u > 0:
                second_lookup(u - 1)
        second_lookup(PACK - 1)

        h_codes = keep.tile([P, O], U32, name="h_codes", align_bytes=64)
        h_scales = keep.tile([P, O], U8, name="h_scales", align_bytes=64)
        for c in range(2):
            places = slice(c * O // 2, (c + 1) * O // 2)
            nc.vector.quantize_mx(
                out=h_codes[:, places].bitcast(FP8X4), scales=h_scales[:, places],
                in_=hid_bf[:, places, :].rearrange("p o u -> p (o u)"),
            )
        for b in range(N // P):
            ns = slice(b * P, (b + 1) * P)
            acc = psum.tile([P, O], F32, name="y%d" % b, tag="bank0_%d" % b)
            nc.tensor.matmul_mx(
                out=acc[:], lhsT=v_codes[:, ns].bitcast(FP4X4), lhsT_scale=v_scales[:, ns],
                rhs=h_codes[:].bitcast(FP8X4), rhs_scale=h_scales[:], start=True, stop=True,
            )
            res = keep.tile([P, O], F32, name="res%d" % b)
            if b == 0:
                nc.vector.tensor_copy(out=res[:], in_=acc[:])
                nc.sync.dma_start(out=out[ns, :], in_=res[:])
            else:
                nc.scalar.copy(out=res[:], in_=acc[:])
                nc.scalar.dma_start(out=out[ns, :], in_=res[:])
